import numpy as np
import ml_dtypes


def mxq(x, axis, fmt="e4m3"):
    dtype, down = {"e4m3": (ml_dtypes.float8_e4m3fn, 7), "e5m2": (ml_dtypes.float8_e5m2, 14)}[fmt]
    v = np.moveaxis(np.asarray(x, np.float32).astype(ml_dtypes.bfloat16).astype(np.float64), axis, -1)
    blocks = v.reshape(v.shape[:-1] + (-1, 32))
    amax = np.abs(blocks).max(-1, keepdims=True)
    byte = np.maximum(np.where(amax > 0, np.frexp(amax)[1] - 1 + 127, 0) - down, 1)
    scale = np.exp2(byte - 127.0)
    codes = (blocks / scale).astype(np.float32).astype(dtype).astype(np.float64)
    return np.moveaxis((codes * scale).reshape(v.shape), -1, axis)


WIDE = False


def mx_kscale(k):
    if not WIDE:
        return np.ones(k)
    levels = np.array([30, -30])
    if k % 512:
        return np.exp2(np.random.permutation(np.resize(levels, k // 32))).repeat(32)
    a = np.empty((k // 512, 16))
    for p in range(k // 512):
        a[p, :8] = np.random.permutation(np.resize(levels, 8))
        for g in range(8):
            far = levels[np.abs(levels - a[p, g]) >= 10]
            a[p, g + 8] = far[np.random.randint(len(far))]
    return np.exp2(a.ravel()).repeat(32)


def f64(x):
    return np.asarray(x).astype(np.float64)


def striped(idx):
    return np.tile(np.asarray(idx).reshape(-1, 16).T, (8, 1)).astype(np.uint16)


def unstriped(offs):
    return offs[:16].T.reshape(-1).astype(np.int64)


E2M1 = np.array([0.0, 0.5, 1.0, 1.5, 2.0, 3.0, 4.0, 6.0, -0.0, -0.5, -1.0, -1.5, -2.0, -3.0, -4.0, -6.0])


def pack_weight(w, fmt):
    k, n = w.shape
    w = f64(np.asarray(w, np.float32).astype(ml_dtypes.bfloat16)).reshape(k // 32, 32, n)
    amax = np.abs(w).max(1)
    if fmt == "e4m3":
        byte = np.frexp(amax)[1] - 1 + 127 - 7
    else:
        mant, ex = np.frexp(amax / 6.0)
        byte = np.where(mant > 0.5, ex, ex - 1) + 127
    byte = np.clip(np.where(amax > 0, byte, 1), 1, 254)
    scaled = (w * np.exp2(127.0 - byte)[:, None, :]).reshape(k, n).astype(np.float32)
    by_word = np.ascontiguousarray(scaled.reshape(k // 512, 128, 4, n).transpose(0, 1, 3, 2))
    if fmt == "e4m3":
        words = by_word.astype(ml_dtypes.float8_e4m3fn).view(np.uint8)
    else:
        c = by_word.astype(ml_dtypes.float4_e2m1fn).view(np.uint8) & 0xF
        words = (c[..., 0::2] | (c[..., 1::2] << 4)).reshape(k // 512, 128, 2 * n)
    return np.ascontiguousarray(words), np.ascontiguousarray(byte.astype(np.uint8).reshape(k // 512, 16, n))


def unpack_weight(words, scales, fmt):
    g, _, n = scales.shape
    words = np.ascontiguousarray(words).reshape(g, 128, n, -1)
    if fmt == "e4m3":
        vals = words.view(ml_dtypes.float8_e4m3fn).astype(np.float64)
    else:
        nib = np.empty((g, 128, n, 4), np.uint8)
        nib[..., 0::2] = words & 0xF
        nib[..., 1::2] = words >> 4
        vals = E2M1[nib]
    vals = vals * np.repeat(np.exp2(scales.astype(np.float64) - 127.0), 8, axis=1)[..., None]
    return vals.transpose(0, 1, 3, 2).reshape(g * 512, n)


K, J, N, R, T, V, C = 512, 512, 256, 256, 1024, 1024, 64


def setup_inputs():
    n = np.random.standard_normal
    idx = np.random.permutation(T)[:J]
    idx2 = np.random.permutation(T)[:J]
    idx3 = np.random.permutation(V)[:J]
    fj = mx_kscale(J)
    fk = mx_kscale(K)
    drp = pack_weight(n((K, R)) * 1 / np.sqrt(K) / fk[:, None], "e4m3")
    return {
        "xf": (n((K, T))).astype(np.float32),
        "ra": (np.random.uniform(0.5, 1.5, (1, J)) * fj).astype(np.float32),
        "gt": (n((N, V)) * np.exp(0.5 * n((1, V)))).astype(np.float32),
        "rb": (np.random.uniform(0.5, 1.5, (1, J)) / fj).astype(np.float32),
        "fkr": (np.random.uniform(0.5, 1.5, (1, K)) * fk).astype(np.float32),
        "dr_words": drp[0],
        "dr_scales": drp[1],
        "old": (12.0 * n((R, N))).astype(np.float32),
        "offs": striped(idx),
        "offs2": striped(idx2),
        "offs3": striped(idx3),
    }


def reference(xf, ra, gt, rb, fkr, dr_words, dr_scales, old, offs, offs2, offs3):
    idx = unstriped(offs)
    idx2 = unstriped(offs2)
    idx3 = unstriped(offs3)
    dru = unpack_weight(dr_words, dr_scales, "e4m3")
    us = np.maximum(f64(xf)[:, idx], f64(xf)[:, idx2]) * f64(ra)
    ut = us.T
    uj = ut * f64(fkr)
    gg = f64(gt)[:, idx3]
    c1 = gg.reshape(N, C, J // C).mean(axis=2)
    c2 = np.repeat(c1, J // C, axis=1)
    gs = (gg - c2) * f64(rb)
    gj = gs.T
    ujq = mxq(uj, 0, "e4m3")
    gjq = mxq(gj, 0, "e5m2")
    w = ujq.T @ gjq
    wq = mxq(w, 0, "e5m2")
    v2 = dru.T @ wq
    y = 0.05 * np.maximum(v2, f64(old))
    return y

@@ -1,0 +1,238 @@
+from contextlib import ExitStack
+
+import concourse.mybir as mybir
+from concourse.masks import make_identity
+
+K, J, N, R, T, V = 512, 512, 256, 256, 1024, 1024
+FLOPS = 2 * J * K * N + 2 * K * R * N
+
+F32 = mybir.dt.float32
+BF16 = mybir.dt.bfloat16
+I32 = mybir.dt.int32
+U32 = mybir.dt.uint32
+U16 = mybir.dt.uint16
+U8 = mybir.dt.uint8
+E4M3 = mybir.dt.float8_e4m3fn_x4
+E5M2 = mybir.dt.float8_e5m2_x4
+ALU = mybir.AluOpType
+COPY = mybir.ActivationFunctionType.Copy
+
+P = 128
+PACK = 4
+SET = 8
+HALVES = N // P
+
+
+def tile_list_directions_larger_centred_larger_kernel(
+    tc, xf, ra, gt, rb, fkr, dr_words, dr_scales, old, offs, offs2, offs3, out
+):
+    nc = tc.nc
+    with ExitStack() as ctx:
+        keep = ctx.enter_context(tc.tile_pool(name="keep", bufs=1))
+        psum = ctx.enter_context(tc.psum_pool(name="psum", bufs=1))
+
+        list1 = keep.tile([P, J // 16], U16, name="list1")
+        list2 = keep.tile([P, J // 16], U16, name="list2")
+        list3 = keep.tile([P, J // 16], U16, name="list3")
+        x_rows = [keep.tile([P, T], F32, name="x_rows%d" % t, align_bytes=64) for t in range(PACK)]
+        g_rows = [keep.tile([P, V], F32, name="g_rows%d" % h) for h in range(HALVES)]
+        ra_col = keep.tile([P, PACK], F32, name="ra_col")
+        rb_col = keep.tile([P, PACK], F32, name="rb_col")
+        fk_col = keep.tile([P, PACK], F32, name="fk_col")
+        dr_codes = keep.tile([P, R], U32, name="dr_codes", align_bytes=64)
+        dr_plane = keep.tile([P, R], U8, name="dr_plane", align_bytes=64)
+        old_rows = keep.tile([P, R // P, N], F32, name="old_rows")
+        ident = keep.tile([P, P], F32, name="ident")
+
+        make_identity(nc, ident[:])
+        nc.gpsimd.memset(dr_plane[:].bitcast(I32), 0)
+
+        x_planes = xf.rearrange("(p t) c -> t p c", t=PACK)
+        nc.sync.dma_start(out=x_rows[0][:], in_=x_planes[0])
+        nc.sync.dma_start(list1[:], offs)
+        nc.sync.dma_start(list2[:], offs2)
+        nc.scalar.dma_start(out=ra_col[:], in_=ra.rearrange("o (p s) -> (o p) s", s=PACK))
+        nc.scalar.dma_start(out=fk_col[:], in_=fkr.rearrange("o (p s) -> (o p) s", s=PACK))
+        nc.sync.dma_start(out=x_rows[1][:], in_=x_planes[1])
+        nc.sync.dma_start(list3[:], offs3)
+        for h in range(HALVES):
+            nc.sync.dma_start(out=g_rows[h][:], in_=gt[h * P : (h + 1) * P, :])
+        for t in range(2, PACK):
+            nc.sync.dma_start(out=x_rows[t][:], in_=x_planes[t])
+        nc.sync.dma_start(out=rb_col[:], in_=rb.rearrange("o (p s) -> (o p) s", s=PACK))
+        nc.sync.dma_start(out=dr_codes[:].bitcast(I32), in_=dr_words[0].rearrange("p c b -> p (c b)").bitcast(I32))
+        for q in range(4):
+            nc.sync.dma_start(
+                out=dr_plane[32 * q : 32 * q + 4, :].bitcast(I32), in_=dr_scales[0, 4 * q : 4 * q + 4, :].bitcast(I32)
+            )
+        nc.sync.dma_start(out=old_rows[:], in_=old.rearrange("(a p) n -> p a n", p=P))
+
+        ra_all = psum.tile([P, PACK, P], F32, name="ra_all")
+        for s in range(PACK):
+            nc.tensor.transpose(ra_all[:, s, :], ra_col[:, s : s + 1].to_broadcast([P, P]), ident[:])
+
+        def gather(engine, dst, window, offsets):
+            if engine == "vector":
+                nc.vector.tensor_copy(out=dst, in_=window.indirect(offsets))
+            else:
+                nc.scalar.activation(out=dst, in_=window.indirect(offsets), func=COPY)
+
+        first = [keep.tile([P, J], F32, name="first%d" % t) for t in range(PACK)]
+        second = [keep.tile([P, J], F32, name="second%d" % t) for t in range(PACK)]
+        larger = [keep.tile([P, J], F32, name="larger%d" % t) for t in range(PACK)]
+        u_rows = [keep.tile([P, J], BF16, name="u_rows%d" % t) for t in range(PACK)]
+        groups = [(0, 1), (2,), (3,)]
+        turned = [psum.tile([P, len(g), 2, P], F32, name="turned%d" % i) for i, g in enumerate(groups)]
+        group_codes = [keep.tile([P, len(g) * P], U32, name="u_codes%d" % i, align_bytes=64) for i, g in enumerate(groups)]
+        group_plane = [keep.tile([P, len(g) * P], U8, name="u_plane%d" % i, align_bytes=64) for i, g in enumerate(groups)]
+        u_codes = [group_codes[i][:, a * P : (a + 1) * P] for i, g in enumerate(groups) for a in range(len(g))]
+        u_plane = [group_plane[i][:, a * P : (a + 1) * P] for i, g in enumerate(groups) for a in range(len(g))]
+        turned_of = [turned[i][:, a] for i, g in enumerate(groups) for a in range(len(g))]
+        u_in = []
+
+        def x_gather(t, engine2, parts=1):
+            for c in range(parts):
+                cols = slice(c * J // parts, (c + 1) * J // parts)
+                entries = slice(cols.start // 16, cols.stop // 16)
+                gather("scalar", first[t][:, cols], x_rows[t][:], list1[:, entries])
+                gather(engine2, second[t][:, cols], x_rows[t][:], list2[:, entries])
+
+        def x_scale(t, parts=1):
+            for c in range(parts):
+                cols = slice(c * J // parts, (c + 1) * J // parts)
+                words = slice(cols.start // PACK, cols.stop // PACK)
+                nc.vector.tensor_tensor(out=larger[t][:, cols], in0=first[t][:, cols], in1=second[t][:, cols], op=ALU.max)
+                nc.vector.scalar_tensor_tensor(
+                    out=u_rows[t][:, cols].rearrange("p (q s) -> p q s", s=PACK),
+                    in0=larger[t][:, cols].rearrange("p (q s) -> p q s", s=PACK),
+                    scalar=fk_col[:, t : t + 1],
+                    in1=ra_all[:, :, words].rearrange("p s q -> p q s"),
+                    op0=ALU.mult,
+                    op1=ALU.mult,
+                )
+            pairs = u_rows[t][:].bitcast(F32)
+            for u in range(2):
+                nc.tensor.transpose(turned_of[t][:, u, :], pairs[:, u::2], ident[:])
+
+        def x_leave(i, tag):
+            planes = len(groups[i])
+            tile = keep.tile([P, planes * P * PACK], BF16, name="u_in", tag=tag, align_bytes=64)
+            nc.scalar.copy(
+                out=tile[:].bitcast(F32).rearrange("q (a p u) -> q a p u", a=planes, u=2),
+                in_=turned[i][:].rearrange("q a u p -> q a p u"),
+            )
+            u_in.append(tile)
+
+        def x_quantise(i):
+            nc.vector.quantize_mx(out=group_codes[i][:].bitcast(E4M3), scales=group_plane[i][:], in_=u_in[i][:])
+
+        picked = [keep.tile([P, J], F32, name="picked%d" % h) for h in range(HALVES)]
+        g_in = keep.tile([P, N, PACK], BF16, name="g_in", align_bytes=64)
+        g_codes = keep.tile([P, N], U32, name="g_codes", align_bytes=64)
+        g_plane = keep.tile([P, N], U8, name="g_plane", align_bytes=64)
+        g_bank = []
+
+        def g_centre(h):
+            sums = keep.tile([P, J // SET], F32, name="sums%d" % h)
+            nc.vector.tensor_reduce(
+                out=sums[:], in_=picked[h][:].rearrange("p (c e) -> p c e", e=SET), axis=mybir.AxisListType.X, op=ALU.add
+            )
+            less = keep.tile([P, J // SET, 2], F32, name="less%d" % h)
+            nc.vector.tensor_scalar(
+                out=less[:],
+                in0=sums[:].unsqueeze(2).to_broadcast([P, J // SET, 2]),
+                scalar1=-1.0 / SET,
+                scalar2=None,
+                op0=ALU.mult,
+            )
+            bank = psum.tile([P, PACK, P], F32, name="g_bank", tag="half%d" % h)
+            for s in range(PACK):
+                nc.tensor.matmul(
+                    bank[:, s, :], lhsT=picked[h][:, s::PACK], rhs=ident[:], is_transpose=True, start=(s == 0), stop=False
+                )
+            for s in range(PACK):
+                nc.tensor.matmul(
+                    bank[:, s, :],
+                    lhsT=less[:].rearrange("p c e -> p (c e)"),
+                    rhs=ident[:],
+                    is_transpose=True,
+                    start=False,
+                    stop=(s == PACK - 1),
+                )
+            g_bank.append(bank)
+
+        def g_scale(h):
+            nc.vector.tensor_tensor(
+                out=g_in[:, h * P : (h + 1) * P, :],
+                in0=g_bank[h][:].rearrange("q s n -> q n s"),
+                in1=rb_col[:].unsqueeze(1).to_broadcast([P, P, PACK]),
+                op=ALU.mult,
+            )
+
+        x_gather(0, "vector")
+        x_scale(0)
+        x_gather(1, "vector")
+        for h in range(HALVES):
+            gather("scalar", picked[h][:], g_rows[h][:], list3[:])
+        x_scale(1)
+        for h in range(HALVES):
+            g_centre(h)
+        x_gather(2, "scalar")
+        x_leave(0, "x_rows2")
+        x_gather(3, "scalar", parts=2)
+        g_scale(0)
+        x_scale(2)
+        g_scale(1)
+        x_quantise(0)
+        x_leave(1, "x_rows3")
+        x_scale(3, parts=2)
+        old_part = keep.tile([P, R // P, N], F32, name="old_part", tag="first%d" % (PACK - 1))
+        nc.scalar.activation(out=old_part[:], in_=old_rows[:], func=COPY, scale=0.05)
+        nc.vector.quantize_mx(
+            out=g_codes[:].bitcast(E5M2), scales=g_plane[:], in_=g_in[:].rearrange("q n s -> q (n s)")
+        )
+        x_quantise(1)
+        x_leave(2, "u_last")
+        x_quantise(2)
+
+        w_bank = [psum.tile([P, PACK, P], F32, name="w_bank%d" % h) for h in range(HALVES)]
+        for t in range(PACK):
+            for h in range(HALVES):
+                cols = slice(h * P, (h + 1) * P)
+                nc.tensor.matmul_mx(
+                    out=w_bank[h][:, t, :],
+                    lhsT=u_codes[t].bitcast(E4M3),
+                    lhsT_scale=u_plane[t],
+                    rhs=g_codes[:, cols].bitcast(E5M2),
+                    rhs_scale=g_plane[:, cols],
+                    start=True,
+                    stop=True,
+                )
+        w_in = [keep.tile([P, P, PACK], BF16, name="w_in%d" % h, align_bytes=64) for h in range(HALVES)]
+        nc.vector.tensor_copy(out=w_in[0][:], in_=w_bank[0][:].rearrange("p t n -> p n t"))
+        nc.scalar.copy(out=w_in[1][:], in_=w_bank[1][:].rearrange("p t n -> p n t"))
+        for h in reversed(range(HALVES)):
+            cols = slice(h * P, (h + 1) * P)
+            w_codes = keep.tile([P, P], U32, name="w_codes%d" % h, align_bytes=64)
+            w_plane = keep.tile([P, P], U8, name="w_plane%d" % h, align_bytes=64)
+            nc.vector.quantize_mx(
+                out=w_codes[:].bitcast(E5M2), scales=w_plane[:], in_=w_in[h][:].rearrange("p n t -> p (n t)")
+            )
+            v_bank = psum.tile([P, R // P, P], F32, name="v_bank", tag="half%d" % h)
+            for a in range(R // P):
+                rows = slice(a * P, (a + 1) * P)
+                nc.tensor.matmul_mx(
+                    out=v_bank[:, a, :],
+                    lhsT=dr_codes[:, rows].bitcast(E4M3),
+                    lhsT_scale=dr_plane[:, rows],
+                    rhs=w_codes[:].bitcast(E5M2),
+                    rhs_scale=w_plane[:],
+                    start=True,
+                    stop=True,
+                )
+            result = keep.tile([P, R // P, P], F32, name="result%d" % h)
+            nc.vector.scalar_tensor_tensor(
+                out=result[:], in0=v_bank[:], scalar=0.05, in1=old_part[:, :, cols], op0=ALU.mult, op1=ALU.max
+            )
+            queue = nc.sync if h == 0 else nc.scalar
+            queue.dma_start(out=out.rearrange("(a p) n -> p a n", p=P)[:, :, cols], in_=result[:])

@@ -44,6 +44,9 @@ def tile_list_directions_larger_centred_larger_kernel(
         old_rows = keep.tile([P, R // P, N], F32, name="old_rows")
         ident = keep.tile([P, P], F32, name="ident")
 
+        warm = keep.tile([P, 2], F32, name="warm")
+        nc.vector.memset(warm[:, 0:1], 0.0)
+        nc.scalar.activation(out=warm[:, 1:2], in_=warm[:, 0:1], func=COPY)
         make_identity(nc, ident[:])
         nc.gpsimd.memset(dr_plane[:].bitcast(I32), 0)
 

@@ -21,6 +21,7 @@ P = 128
 PACK = 4
 SET = 8
 HALVES = N // P
+LAST_CUT = 384
 
 
 def tile_list_directions_larger_centred_larger_kernel(
@@ -56,13 +57,13 @@ def tile_list_directions_larger_centred_larger_kernel(
         nc.sync.dma_start(list2[:], offs2)
         nc.scalar.dma_start(out=ra_col[:], in_=ra.rearrange("o (p s) -> (o p) s", s=PACK))
         nc.scalar.dma_start(out=fk_col[:], in_=fkr.rearrange("o (p s) -> (o p) s", s=PACK))
-        nc.sync.dma_start(out=x_rows[1][:], in_=x_planes[1])
+        nc.sync.dma_start(out=g_rows[0][:], in_=gt[0:P, :])
         nc.sync.dma_start(list3[:], offs3)
-        for h in range(HALVES):
-            nc.sync.dma_start(out=g_rows[h][:], in_=gt[h * P : (h + 1) * P, :])
+        nc.sync.dma_start(out=g_rows[1][:], in_=gt[P : 2 * P, :])
+        nc.sync.dma_start(out=x_rows[1][:], in_=x_planes[1])
+        nc.sync.dma_start(out=rb_col[:], in_=rb.rearrange("o (p s) -> (o p) s", s=PACK))
         for t in range(2, PACK):
             nc.sync.dma_start(out=x_rows[t][:], in_=x_planes[t])
-        nc.sync.dma_start(out=rb_col[:], in_=rb.rearrange("o (p s) -> (o p) s", s=PACK))
         nc.sync.dma_start(out=dr_codes[:].bitcast(I32), in_=dr_words[0].rearrange("p c b -> p (c b)").bitcast(I32))
         for q in range(4):
             nc.sync.dma_start(
@@ -80,39 +81,40 @@ def tile_list_directions_larger_centred_larger_kernel(
             else:
                 nc.scalar.activation(out=dst, in_=window.indirect(offsets), func=COPY)
 
-        first = [keep.tile([P, J], F32, name="first%d" % t) for t in range(PACK)]
+        first = [keep.tile([P, J], F32, name="first%d" % t, align_bytes=64) for t in range(PACK)]
         second = [keep.tile([P, J], F32, name="second%d" % t) for t in range(PACK)]
-        larger = [keep.tile([P, J], F32, name="larger%d" % t) for t in range(PACK)]
+        larger = {}
         u_rows = [keep.tile([P, J], BF16, name="u_rows%d" % t) for t in range(PACK)]
         groups = [(0, 1), (2,), (3,)]
         turned = [psum.tile([P, len(g), 2, P], F32, name="turned%d" % i) for i, g in enumerate(groups)]
-        group_codes = [keep.tile([P, len(g) * P], U32, name="u_codes%d" % i, align_bytes=64) for i, g in enumerate(groups)]
+        u_codes = []
         group_plane = [keep.tile([P, len(g) * P], U8, name="u_plane%d" % i, align_bytes=64) for i, g in enumerate(groups)]
-        u_codes = [group_codes[i][:, a * P : (a + 1) * P] for i, g in enumerate(groups) for a in range(len(g))]
         u_plane = [group_plane[i][:, a * P : (a + 1) * P] for i, g in enumerate(groups) for a in range(len(g))]
         turned_of = [turned[i][:, a] for i, g in enumerate(groups) for a in range(len(g))]
         u_in = []
 
-        def x_gather(t, engine2, parts=1):
-            for c in range(parts):
-                cols = slice(c * J // parts, (c + 1) * J // parts)
-                entries = slice(cols.start // 16, cols.stop // 16)
-                gather("scalar", first[t][:, cols], x_rows[t][:], list1[:, entries])
-                gather(engine2, second[t][:, cols], x_rows[t][:], list2[:, entries])
+        def x_gather(t, engine2, cols=slice(0, J)):
+            entries = slice(cols.start // 16, cols.stop // 16)
+            gather("scalar", first[t][:, cols], x_rows[t][:], list1[:, entries])
+            gather(engine2, second[t][:, cols], x_rows[t][:], list2[:, entries])
 
-        def x_scale(t, parts=1):
-            for c in range(parts):
-                cols = slice(c * J // parts, (c + 1) * J // parts)
-                words = slice(cols.start // PACK, cols.stop // PACK)
-                nc.vector.tensor_tensor(out=larger[t][:, cols], in0=first[t][:, cols], in1=second[t][:, cols], op=ALU.max)
-                nc.vector.scalar_tensor_tensor(
-                    out=u_rows[t][:, cols].rearrange("p (q s) -> p q s", s=PACK),
-                    in0=larger[t][:, cols].rearrange("p (q s) -> p q s", s=PACK),
-                    scalar=fk_col[:, t : t + 1],
-                    in1=ra_all[:, :, words].rearrange("p s q -> p q s"),
-                    op0=ALU.mult,
-                    op1=ALU.mult,
-                )
+        def x_max(t, tag, cols=slice(0, J)):
+            tile = keep.tile([P, cols.stop - cols.start], F32, name="larger", tag=tag, align_bytes=64)
+            larger.setdefault((t, cols.start), tile)
+            nc.vector.tensor_tensor(out=tile[:], in0=first[t][:, cols], in1=second[t][:, cols], op=ALU.max)
+
+        def x_scale(t, cols=slice(0, J)):
+            words = slice(cols.start // PACK, cols.stop // PACK)
+            nc.vector.scalar_tensor_tensor(
+                out=u_rows[t][:, cols].rearrange("p (q s) -> p q s", s=PACK),
+                in0=larger[(t, cols.start)][:].rearrange("p (q s) -> p q s", s=PACK),
+                scalar=fk_col[:, t : t + 1],
+                in1=ra_all[:, :, words].rearrange("p s q -> p q s"),
+                op0=ALU.mult,
+                op1=ALU.mult,
+            )
+
+        def x_turn(t):
             pairs = u_rows[t][:].bitcast(F32)
             for u in range(2):
                 nc.tensor.transpose(turned_of[t][:, u, :], pairs[:, u::2], ident[:])
@@ -126,27 +128,31 @@ def tile_list_directions_larger_centred_larger_kernel(
             )
             u_in.append(tile)
 
-        def x_quantise(i):
-            nc.vector.quantize_mx(out=group_codes[i][:].bitcast(E4M3), scales=group_plane[i][:], in_=u_in[i][:])
+        def x_quantise(i, tag):
+            planes = len(groups[i])
+            codes = keep.tile([P, planes * P], U32, name="u_codes", tag=tag, align_bytes=64)
+            nc.vector.quantize_mx(out=codes[:].bitcast(E4M3), scales=group_plane[i][:], in_=u_in[i][:])
+            u_codes.extend([codes[:, a * P : (a + 1) * P] for a in range(planes)])
 
         picked = [keep.tile([P, J], F32, name="picked%d" % h) for h in range(HALVES)]
-        g_in = keep.tile([P, N, PACK], BF16, name="g_in", align_bytes=64)
+        g_in = []
         g_codes = keep.tile([P, N], U32, name="g_codes", align_bytes=64)
         g_plane = keep.tile([P, N], U8, name="g_plane", align_bytes=64)
         g_bank = []
 
-        def g_centre(h):
-            sums = keep.tile([P, J // SET], F32, name="sums%d" % h)
+        def g_centre(h, tag):
+            sums = keep.tile([P, J // SET], F32, name="sums", tag=tag, align_bytes=64)
             nc.vector.tensor_reduce(
                 out=sums[:], in_=picked[h][:].rearrange("p (c e) -> p c e", e=SET), axis=mybir.AxisListType.X, op=ALU.add
             )
             less = keep.tile([P, J // SET, 2], F32, name="less%d" % h)
-            nc.vector.tensor_scalar(
+            nc.gpsimd.tensor_scalar(
                 out=less[:],
                 in0=sums[:].unsqueeze(2).to_broadcast([P, J // SET, 2]),
                 scalar1=-1.0 / SET,
-                scalar2=None,
+                scalar2=0.0,
                 op0=ALU.mult,
+                op1=ALU.add,
             )
             bank = psum.tile([P, PACK, P], F32, name="g_bank", tag="half%d" % h)
             for s in range(PACK):
@@ -164,39 +170,57 @@ def tile_list_directions_larger_centred_larger_kernel(
                 )
             g_bank.append(bank)
 
-        def g_scale(h):
+        def g_quantise(h):
+            cols = slice(h * P, (h + 1) * P)
+            nc.vector.quantize_mx(
+                out=g_codes[:, cols].bitcast(E5M2), scales=g_plane[:, cols], in_=g_in[h][:].rearrange("q n s -> q (n s)")
+            )
+
+        def g_scale(h, tag):
+            g_in.append(keep.tile([P, P, PACK], BF16, name="g_in", tag=tag, align_bytes=64))
             nc.vector.tensor_tensor(
-                out=g_in[:, h * P : (h + 1) * P, :],
+                out=g_in[h][:],
                 in0=g_bank[h][:].rearrange("q s n -> q n s"),
                 in1=rb_col[:].unsqueeze(1).to_broadcast([P, P, PACK]),
                 op=ALU.mult,
             )
 
+        early, late = slice(0, LAST_CUT), slice(LAST_CUT, J)
         x_gather(0, "vector")
+        x_max(0, "larger0")
         x_scale(0)
-        x_gather(1, "vector")
+        x_turn(0)
         for h in range(HALVES):
             gather("scalar", picked[h][:], g_rows[h][:], list3[:])
+        g_centre(0, "sums0")
+        x_gather(1, "vector")
+        g_centre(1, "x_rows1")
+        x_max(1, "larger1")
+        g_scale(0, "g_in0")
         x_scale(1)
-        for h in range(HALVES):
-            g_centre(h)
+        x_turn(1)
         x_gather(2, "scalar")
-        x_leave(0, "x_rows2")
-        x_gather(3, "scalar", parts=2)
-        g_scale(0)
+        x_gather(3, "scalar", early)
+        x_gather(3, "scalar", late)
+        g_scale(1, "g_in1")
+        x_max(2, "larger2")
+        g_quantise(0)
         x_scale(2)
-        g_scale(1)
-        x_quantise(0)
-        x_leave(1, "x_rows3")
-        x_scale(3, parts=2)
-        old_part = keep.tile([P, R // P, N], F32, name="old_part", tag="first%d" % (PACK - 1))
+        x_turn(2)
+        x_leave(0, "x_rows3")
+        x_max(3, "larger3", early)
+        g_quantise(1)
+        x_scale(3, early)
+        x_max(3, "larger_last", late)
+        x_scale(3, late)
+        x_turn(3)
+        x_leave(1, "first3")
+        old_part = keep.tile([P, R // P, N], F32, name="old_part", tag="fk_col")
         nc.scalar.activation(out=old_part[:], in_=old_rows[:], func=COPY, scale=0.05)
-        nc.vector.quantize_mx(
-            out=g_codes[:].bitcast(E5M2), scales=g_plane[:], in_=g_in[:].rearrange("q n s -> q (n s)")
-        )
-        x_quantise(1)
+        x_quantise(0, "larger_last")
+        x_quantise(1, "u_codes1")
         x_leave(2, "u_last")
-        x_quantise(2)
+        x_quantise(2, "u_codes2")
 
         w_bank = [psum.tile([P, PACK, P], F32, name="w_bank%d" % h) for h in range(HALVES)]
         for t in range(PACK):

@@ -22,6 +22,7 @@ PACK = 4
 SET = 8
 HALVES = N // P
 LAST_CUT = 384
+G_CUT = 128
 
 
 def tile_list_directions_larger_centred_larger_kernel(
@@ -36,7 +37,7 @@ def tile_list_directions_larger_centred_larger_kernel(
         list2 = keep.tile([P, J // 16], U16, name="list2")
         list3 = keep.tile([P, J // 16], U16, name="list3")
         x_rows = [keep.tile([P, T], F32, name="x_rows%d" % t, align_bytes=64) for t in range(PACK)]
-        g_rows = [keep.tile([P, V], F32, name="g_rows%d" % h) for h in range(HALVES)]
+        g_rows = [keep.tile([P, V], F32, name="g_rows%d" % h, align_bytes=64) for h in range(HALVES)]
         ra_col = keep.tile([P, PACK], F32, name="ra_col")
         rb_col = keep.tile([P, PACK], F32, name="rb_col")
         fk_col = keep.tile([P, PACK], F32, name="fk_col")
@@ -57,10 +58,10 @@ def tile_list_directions_larger_centred_larger_kernel(
         nc.sync.dma_start(list2[:], offs2)
         nc.scalar.dma_start(out=ra_col[:], in_=ra.rearrange("o (p s) -> (o p) s", s=PACK))
         nc.scalar.dma_start(out=fk_col[:], in_=fkr.rearrange("o (p s) -> (o p) s", s=PACK))
+        nc.sync.dma_start(out=x_rows[1][:], in_=x_planes[1])
         nc.sync.dma_start(out=g_rows[0][:], in_=gt[0:P, :])
         nc.sync.dma_start(list3[:], offs3)
         nc.sync.dma_start(out=g_rows[1][:], in_=gt[P : 2 * P, :])
-        nc.sync.dma_start(out=x_rows[1][:], in_=x_planes[1])
         nc.sync.dma_start(out=rb_col[:], in_=rb.rearrange("o (p s) -> (o p) s", s=PACK))
         for t in range(2, PACK):
             nc.sync.dma_start(out=x_rows[t][:], in_=x_planes[t])
@@ -140,11 +141,15 @@ def tile_list_directions_larger_centred_larger_kernel(
         g_plane = keep.tile([P, N], U8, name="g_plane", align_bytes=64)
         g_bank = []
 
-        def g_centre(h, tag):
-            sums = keep.tile([P, J // SET], F32, name="sums", tag=tag, align_bytes=64)
-            nc.vector.tensor_reduce(
-                out=sums[:], in_=picked[h][:].rearrange("p (c e) -> p c e", e=SET), axis=mybir.AxisListType.X, op=ALU.add
-            )
+        def g_centre(h, pieces):
+            sums = keep.tile([P, J // SET], F32, name="sums%d" % h)
+            for cols in pieces:
+                nc.vector.tensor_reduce(
+                    out=sums[:, cols.start // SET : cols.stop // SET],
+                    in_=picked[h][:, cols].rearrange("p (c e) -> p c e", e=SET),
+                    axis=mybir.AxisListType.X,
+                    op=ALU.add,
+                )
             less = keep.tile([P, J // SET, 2], F32, name="less%d" % h)
             nc.gpsimd.tensor_scalar(
                 out=less[:],
@@ -190,28 +195,30 @@ def tile_list_directions_larger_centred_larger_kernel(
         x_max(0, "larger0")
         x_scale(0)
         x_turn(0)
-        for h in range(HALVES):
-            gather("scalar", picked[h][:], g_rows[h][:], list3[:])
-        g_centre(0, "sums0")
-        x_gather(1, "vector")
-        g_centre(1, "x_rows1")
-        x_max(1, "larger1")
-        g_scale(0, "g_in0")
+        x_gather(1, "scalar")
+        head, rest = slice(0, G_CUT), slice(G_CUT, J)
+        for cols in (head, rest):
+            gather("vector", picked[0][:, cols], g_rows[0][:], list3[:, cols.start // 16 : cols.stop // 16])
+        g_centre(0, (head, rest))
+        gather("scalar", picked[1][:], g_rows[1][:], list3[:])
+        x_max(1, "g_rows0")
+        g_centre(1, (slice(0, J),))
         x_scale(1)
         x_turn(1)
+        g_scale(0, "g_in0")
         x_gather(2, "scalar")
         x_gather(3, "scalar", early)
         x_gather(3, "scalar", late)
-        g_scale(1, "g_in1")
         x_max(2, "larger2")
-        g_quantise(0)
+        g_scale(1, "first2")
         x_scale(2)
         x_turn(2)
         x_leave(0, "x_rows3")
         x_max(3, "larger3", early)
-        g_quantise(1)
+        g_quantise(0)
         x_scale(3, early)
         x_max(3, "larger_last", late)
+        g_quantise(1)
         x_scale(3, late)
         x_turn(3)
         x_leave(1, "first3")
@@ -245,11 +252,11 @@ def tile_list_directions_larger_centred_larger_kernel(
             nc.vector.quantize_mx(
                 out=w_codes[:].bitcast(E5M2), scales=w_plane[:], in_=w_in[h][:].rearrange("p n t -> p (n t)")
             )
-            v_bank = psum.tile([P, R // P, P], F32, name="v_bank", tag="half%d" % h)
             for a in range(R // P):
                 rows = slice(a * P, (a + 1) * P)
+                v_bank = psum.tile([P, P], F32, name="v_bank", tag=("half%d", "turned%d")[a] % h)
                 nc.tensor.matmul_mx(
-                    out=v_bank[:, a, :],
+                    out=v_bank[:],
                     lhsT=dr_codes[:, rows].bitcast(E4M3),
                     lhsT_scale=dr_plane[:, rows],
                     rhs=w_codes[:].bitcast(E5M2),
@@ -257,9 +264,9 @@ def tile_list_directions_larger_centred_larger_kernel(
                     start=True,
                     stop=True,
                 )
-            result = keep.tile([P, R // P, P], F32, name="result%d" % h)
-            nc.vector.scalar_tensor_tensor(
-                out=result[:], in0=v_bank[:], scalar=0.05, in1=old_part[:, :, cols], op0=ALU.mult, op1=ALU.max
-            )
-            queue = nc.sync if h == 0 else nc.scalar
-            queue.dma_start(out=out.rearrange("(a p) n -> p a n", p=P)[:, :, cols], in_=result[:])
+                result = keep.tile([P, P], F32, name="result%d%d" % (h, a))
+                nc.vector.scalar_tensor_tensor(
+                    out=result[:], in0=v_bank[:], scalar=0.05, in1=old_part[:, a, cols], op0=ALU.mult, op1=ALU.max
+                )
+                queue = nc.sync if a == 0 else nc.scalar
+                queue.dma_start(out=out[rows, cols], in_=result[:])

@@ -20,9 +20,14 @@ COPY = mybir.ActivationFunctionType.Copy
 P = 128
 PACK = 4
 SET = 8
+STRIPE = 16
+QUADRANT = 32
 HALVES = N // P
+ALL_SLOTS = slice(0, J)
+OUT_SCALE = 0.05
 LAST_CUT = 384
 G_CUT = 128
+GROUPS = ((0, 1), (2,), (3,))
 
 
 def tile_list_directions_larger_centred_larger_kernel(
@@ -33,9 +38,9 @@ def tile_list_directions_larger_centred_larger_kernel(
         keep = ctx.enter_context(tc.tile_pool(name="keep", bufs=1))
         psum = ctx.enter_context(tc.psum_pool(name="psum", bufs=1))
 
-        list1 = keep.tile([P, J // 16], U16, name="list1")
-        list2 = keep.tile([P, J // 16], U16, name="list2")
-        list3 = keep.tile([P, J // 16], U16, name="list3")
+        list1 = keep.tile([P, J // STRIPE], U16, name="list1")
+        list2 = keep.tile([P, J // STRIPE], U16, name="list2")
+        list3 = keep.tile([P, J // STRIPE], U16, name="list3")
         x_rows = [keep.tile([P, T], F32, name="x_rows%d" % t, align_bytes=64) for t in range(PACK)]
         g_rows = [keep.tile([P, V], F32, name="g_rows%d" % h, align_bytes=64) for h in range(HALVES)]
         ra_col = keep.tile([P, PACK], F32, name="ra_col")
@@ -56,19 +61,20 @@ def tile_list_directions_larger_centred_larger_kernel(
         nc.sync.dma_start(out=x_rows[0][:], in_=x_planes[0])
         nc.sync.dma_start(list1[:], offs)
         nc.sync.dma_start(list2[:], offs2)
-        nc.scalar.dma_start(out=ra_col[:], in_=ra.rearrange("o (p s) -> (o p) s", s=PACK))
-        nc.scalar.dma_start(out=fk_col[:], in_=fkr.rearrange("o (p s) -> (o p) s", s=PACK))
+        nc.sync.dma_start(out=ra_col[:], in_=ra.rearrange("o (p s) -> (o p) s", s=PACK))
+        nc.sync.dma_start(out=fk_col[:], in_=fkr.rearrange("o (p s) -> (o p) s", s=PACK))
         nc.sync.dma_start(out=x_rows[1][:], in_=x_planes[1])
-        nc.sync.dma_start(out=g_rows[0][:], in_=gt[0:P, :])
         nc.sync.dma_start(list3[:], offs3)
+        nc.sync.dma_start(out=g_rows[0][:], in_=gt[0:P, :])
         nc.sync.dma_start(out=g_rows[1][:], in_=gt[P : 2 * P, :])
+        nc.sync.dma_start(out=x_rows[2][:], in_=x_planes[2])
         nc.sync.dma_start(out=rb_col[:], in_=rb.rearrange("o (p s) -> (o p) s", s=PACK))
-        for t in range(2, PACK):
-            nc.sync.dma_start(out=x_rows[t][:], in_=x_planes[t])
+        nc.sync.dma_start(out=x_rows[3][:], in_=x_planes[3])
         nc.sync.dma_start(out=dr_codes[:].bitcast(I32), in_=dr_words[0].rearrange("p c b -> p (c b)").bitcast(I32))
-        for q in range(4):
+        for q in range(P // QUADRANT):
             nc.sync.dma_start(
-                out=dr_plane[32 * q : 32 * q + 4, :].bitcast(I32), in_=dr_scales[0, 4 * q : 4 * q + 4, :].bitcast(I32)
+                out=dr_plane[QUADRANT * q : QUADRANT * q + PACK, :].bitcast(I32),
+                in_=dr_scales[0, PACK * q : PACK * (q + 1), :].bitcast(I32),
             )
         nc.sync.dma_start(out=old_rows[:], in_=old.rearrange("(a p) n -> p a n", p=P))
 
@@ -76,41 +82,42 @@ def tile_list_directions_larger_centred_larger_kernel(
         for s in range(PACK):
             nc.tensor.transpose(ra_all[:, s, :], ra_col[:, s : s + 1].to_broadcast([P, P]), ident[:])
 
-        def gather(engine, dst, window, offsets):
-            if engine == "vector":
-                nc.vector.tensor_copy(out=dst, in_=window.indirect(offsets))
-            else:
-                nc.scalar.activation(out=dst, in_=window.indirect(offsets), func=COPY)
+        def entries(list_tile, slots):
+            return list_tile[:, slots.start // STRIPE : slots.stop // STRIPE]
+
+        def vector_gather(dst, window, list_tile, slots):
+            nc.vector.tensor_copy(out=dst[:, slots], in_=window[:].indirect(entries(list_tile, slots)))
+
+        def scalar_gather(dst, window, list_tile, slots):
+            nc.scalar.activation(out=dst[:, slots], in_=window[:].indirect(entries(list_tile, slots)), func=COPY)
 
         first = [keep.tile([P, J], F32, name="first%d" % t, align_bytes=64) for t in range(PACK)]
         second = [keep.tile([P, J], F32, name="second%d" % t) for t in range(PACK)]
         larger = {}
         u_rows = [keep.tile([P, J], BF16, name="u_rows%d" % t) for t in range(PACK)]
-        groups = [(0, 1), (2,), (3,)]
-        turned = [psum.tile([P, len(g), 2, P], F32, name="turned%d" % i) for i, g in enumerate(groups)]
+        turned = [psum.tile([P, len(g), 2, P], F32, name="turned%d" % i) for i, g in enumerate(GROUPS)]
         u_codes = []
-        group_plane = [keep.tile([P, len(g) * P], U8, name="u_plane%d" % i, align_bytes=64) for i, g in enumerate(groups)]
-        u_plane = [group_plane[i][:, a * P : (a + 1) * P] for i, g in enumerate(groups) for a in range(len(g))]
-        turned_of = [turned[i][:, a] for i, g in enumerate(groups) for a in range(len(g))]
+        group_plane = [keep.tile([P, len(g) * P], U8, name="u_plane%d" % i, align_bytes=64) for i, g in enumerate(GROUPS)]
+        u_plane = [group_plane[i][:, a * P : (a + 1) * P] for i, g in enumerate(GROUPS) for a in range(len(g))]
+        turned_of = [turned[i][:, a] for i, g in enumerate(GROUPS) for a in range(len(g))]
         u_in = []
 
-        def x_gather(t, engine2, cols=slice(0, J)):
-            entries = slice(cols.start // 16, cols.stop // 16)
-            gather("scalar", first[t][:, cols], x_rows[t][:], list1[:, entries])
-            gather(engine2, second[t][:, cols], x_rows[t][:], list2[:, entries])
+        def x_gather(t, second_gather, slots=ALL_SLOTS):
+            scalar_gather(first[t], x_rows[t], list1, slots)
+            second_gather(second[t], x_rows[t], list2, slots)
 
-        def x_max(t, tag, cols=slice(0, J)):
-            tile = keep.tile([P, cols.stop - cols.start], F32, name="larger", tag=tag, align_bytes=64)
-            larger.setdefault((t, cols.start), tile)
-            nc.vector.tensor_tensor(out=tile[:], in0=first[t][:, cols], in1=second[t][:, cols], op=ALU.max)
+        def x_max(t, tag, slots=ALL_SLOTS):
+            tile = keep.tile([P, slots.stop - slots.start], F32, name="larger", tag=tag, align_bytes=64)
+            larger[(t, slots.start)] = tile
+            nc.vector.tensor_tensor(out=tile[:], in0=first[t][:, slots], in1=second[t][:, slots], op=ALU.max)
 
-        def x_scale(t, cols=slice(0, J)):
-            words = slice(cols.start // PACK, cols.stop // PACK)
+        def x_scale(t, slots=ALL_SLOTS):
+            quads = slice(slots.start // PACK, slots.stop // PACK)
             nc.vector.scalar_tensor_tensor(
-                out=u_rows[t][:, cols].rearrange("p (q s) -> p q s", s=PACK),
-                in0=larger[(t, cols.start)][:].rearrange("p (q s) -> p q s", s=PACK),
+                out=u_rows[t][:, slots].rearrange("p (q s) -> p q s", s=PACK),
+                in0=larger[(t, slots.start)][:].rearrange("p (q s) -> p q s", s=PACK),
                 scalar=fk_col[:, t : t + 1],
-                in1=ra_all[:, :, words].rearrange("p s q -> p q s"),
+                in1=ra_all[:, :, quads].rearrange("p s q -> p q s"),
                 op0=ALU.mult,
                 op1=ALU.mult,
             )
@@ -121,7 +128,7 @@ def tile_list_directions_larger_centred_larger_kernel(
                 nc.tensor.transpose(turned_of[t][:, u, :], pairs[:, u::2], ident[:])
 
         def x_leave(i, tag):
-            planes = len(groups[i])
+            planes = len(GROUPS[i])
             tile = keep.tile([P, planes * P * PACK], BF16, name="u_in", tag=tag, align_bytes=64)
             nc.scalar.copy(
                 out=tile[:].bitcast(F32).rearrange("q (a p u) -> q a p u", a=planes, u=2),
@@ -130,7 +137,7 @@ def tile_list_directions_larger_centred_larger_kernel(
             u_in.append(tile)
 
         def x_quantise(i, tag):
-            planes = len(groups[i])
+            planes = len(GROUPS[i])
             codes = keep.tile([P, planes * P], U32, name="u_codes", tag=tag, align_bytes=64)
             nc.vector.quantize_mx(out=codes[:].bitcast(E4M3), scales=group_plane[i][:], in_=u_in[i][:])
             u_codes.extend([codes[:, a * P : (a + 1) * P] for a in range(planes)])
@@ -143,17 +150,17 @@ def tile_list_directions_larger_centred_larger_kernel(
 
         def g_centre(h, pieces):
             sums = keep.tile([P, J // SET], F32, name="sums%d" % h)
-            for cols in pieces:
+            for slots in pieces:
                 nc.vector.tensor_reduce(
-                    out=sums[:, cols.start // SET : cols.stop // SET],
-                    in_=picked[h][:, cols].rearrange("p (c e) -> p c e", e=SET),
+                    out=sums[:, slots.start // SET : slots.stop // SET],
+                    in_=picked[h][:, slots].rearrange("p (c e) -> p c e", e=SET),
                     axis=mybir.AxisListType.X,
                     op=ALU.add,
                 )
-            less = keep.tile([P, J // SET, 2], F32, name="less%d" % h)
+            less = keep.tile([P, J // SET, SET // PACK], F32, name="less%d" % h)
             nc.gpsimd.tensor_scalar(
                 out=less[:],
-                in0=sums[:].unsqueeze(2).to_broadcast([P, J // SET, 2]),
+                in0=sums[:].unsqueeze(2).to_broadcast([P, J // SET, SET // PACK]),
                 scalar1=-1.0 / SET,
                 scalar2=0.0,
                 op0=ALU.mult,
@@ -191,24 +198,24 @@ def tile_list_directions_larger_centred_larger_kernel(
             )
 
         early, late = slice(0, LAST_CUT), slice(LAST_CUT, J)
-        x_gather(0, "vector")
+        head, rest = slice(0, G_CUT), slice(G_CUT, J)
+        x_gather(0, vector_gather)
         x_max(0, "larger0")
         x_scale(0)
         x_turn(0)
-        x_gather(1, "scalar")
-        head, rest = slice(0, G_CUT), slice(G_CUT, J)
-        for cols in (head, rest):
-            gather("vector", picked[0][:, cols], g_rows[0][:], list3[:, cols.start // 16 : cols.stop // 16])
+        x_gather(1, scalar_gather)
+        for slots in (head, rest):
+            vector_gather(picked[0], g_rows[0], list3, slots)
         g_centre(0, (head, rest))
-        gather("scalar", picked[1][:], g_rows[1][:], list3[:])
+        scalar_gather(picked[1], g_rows[1], list3, ALL_SLOTS)
         x_max(1, "g_rows0")
-        g_centre(1, (slice(0, J),))
+        g_centre(1, (ALL_SLOTS,))
         x_scale(1)
         x_turn(1)
         g_scale(0, "g_in0")
-        x_gather(2, "scalar")
-        x_gather(3, "scalar", early)
-        x_gather(3, "scalar", late)
+        x_gather(2, scalar_gather)
+        x_gather(3, scalar_gather, early)
+        x_gather(3, scalar_gather, late)
         x_max(2, "larger2")
         g_scale(1, "first2")
         x_scale(2)
@@ -223,7 +230,7 @@ def tile_list_directions_larger_centred_larger_kernel(
         x_turn(3)
         x_leave(1, "first3")
         old_part = keep.tile([P, R // P, N], F32, name="old_part", tag="fk_col")
-        nc.scalar.activation(out=old_part[:], in_=old_rows[:], func=COPY, scale=0.05)
+        nc.scalar.activation(out=old_part[:], in_=old_rows[:], func=COPY, scale=OUT_SCALE)
         x_quantise(0, "larger_last")
         x_quantise(1, "u_codes1")
         x_leave(2, "u_last")
@@ -266,7 +273,6 @@ def tile_list_directions_larger_centred_larger_kernel(
                 )
                 result = keep.tile([P, P], F32, name="result%d%d" % (h, a))
                 nc.vector.scalar_tensor_tensor(
-                    out=result[:], in0=v_bank[:], scalar=0.05, in1=old_part[:, a, cols], op0=ALU.mult, op1=ALU.max
+                    out=result[:], in0=v_bank[:], scalar=OUT_SCALE, in1=old_part[:, a, cols], op0=ALU.mult, op1=ALU.max
                 )
-                queue = nc.sync if a == 0 else nc.scalar
-                queue.dma_start(out=out[rows, cols], in_=result[:])
+                (nc.sync, nc.scalar)[a].dma_start(out=out[rows, cols], in_=result[:])

from contextlib import ExitStack

import concourse.mybir as mybir
from concourse.masks import make_identity

K, J, N, R, T, V = 512, 512, 256, 256, 1024, 1024
FLOPS = 2 * J * K * N + 2 * K * R * N

F32 = mybir.dt.float32
BF16 = mybir.dt.bfloat16
I32 = mybir.dt.int32
U32 = mybir.dt.uint32
U16 = mybir.dt.uint16
U8 = mybir.dt.uint8
E4M3 = mybir.dt.float8_e4m3fn_x4
E5M2 = mybir.dt.float8_e5m2_x4
ALU = mybir.AluOpType
COPY = mybir.ActivationFunctionType.Copy

P = 128
PACK = 4
SET = 8
STRIPE = 16
QUADRANT = 32
HALVES = N // P
ALL_SLOTS = slice(0, J)
OUT_SCALE = 0.05
LAST_CUT = 384
G_CUT = 128
GROUPS = ((0, 1), (2,), (3,))


def tile_list_directions_larger_centred_larger_kernel(
    tc, xf, ra, gt, rb, fkr, dr_words, dr_scales, old, offs, offs2, offs3, out
):
    nc = tc.nc
    with ExitStack() as ctx:
        keep = ctx.enter_context(tc.tile_pool(name="keep", bufs=1))
        psum = ctx.enter_context(tc.psum_pool(name="psum", bufs=1))

        list1 = keep.tile([P, J // STRIPE], U16, name="list1")
        list2 = keep.tile([P, J // STRIPE], U16, name="list2")
        list3 = keep.tile([P, J // STRIPE], U16, name="list3")
        x_rows = [keep.tile([P, T], F32, name="x_rows%d" % t, align_bytes=64) for t in range(PACK)]
        g_rows = [keep.tile([P, V], F32, name="g_rows%d" % h, align_bytes=64) for h in range(HALVES)]
        ra_col = keep.tile([P, PACK], F32, name="ra_col")
        rb_col = keep.tile([P, PACK], F32, name="rb_col")
        fk_col = keep.tile([P, PACK], F32, name="fk_col")
        dr_codes = keep.tile([P, R], U32, name="dr_codes", align_bytes=64)
        dr_plane = keep.tile([P, R], U8, name="dr_plane", align_bytes=64)
        old_rows = keep.tile([P, R // P, N], F32, name="old_rows")
        ident = keep.tile([P, P], F32, name="ident")

        warm = keep.tile([P, 2], F32, name="warm")
        nc.vector.memset(warm[:, 0:1], 0.0)
        nc.scalar.activation(out=warm[:, 1:2], in_=warm[:, 0:1], func=COPY)
        make_identity(nc, ident[:])
        nc.gpsimd.memset(dr_plane[:].bitcast(I32), 0)

        x_planes = xf.rearrange("(p t) c -> t p c", t=PACK)
        nc.sync.dma_start(out=x_rows[0][:], in_=x_planes[0])
        nc.sync.dma_start(list1[:], offs)
        nc.sync.dma_start(list2[:], offs2)
        nc.sync.dma_start(out=ra_col[:], in_=ra.rearrange("o (p s) -> (o p) s", s=PACK))
        nc.sync.dma_start(out=fk_col[:], in_=fkr.rearrange("o (p s) -> (o p) s", s=PACK))
        nc.sync.dma_start(out=x_rows[1][:], in_=x_planes[1])
        nc.sync.dma_start(list3[:], offs3)
        nc.sync.dma_start(out=g_rows[0][:], in_=gt[0:P, :])
        nc.sync.dma_start(out=g_rows[1][:], in_=gt[P : 2 * P, :])
        nc.sync.dma_start(out=x_rows[2][:], in_=x_planes[2])
        nc.sync.dma_start(out=rb_col[:], in_=rb.rearrange("o (p s) -> (o p) s", s=PACK))
        nc.sync.dma_start(out=x_rows[3][:], in_=x_planes[3])
        nc.sync.dma_start(out=dr_codes[:].bitcast(I32), in_=dr_words[0].rearrange("p c b -> p (c b)").bitcast(I32))
        for q in range(P // QUADRANT):
            nc.sync.dma_start(
                out=dr_plane[QUADRANT * q : QUADRANT * q + PACK, :].bitcast(I32),
                in_=dr_scales[0, PACK * q : PACK * (q + 1), :].bitcast(I32),
            )
        nc.sync.dma_start(out=old_rows[:], in_=old.rearrange("(a p) n -> p a n", p=P))

        ra_all = psum.tile([P, PACK, P], F32, name="ra_all")
        for s in range(PACK):
            nc.tensor.transpose(ra_all[:, s, :], ra_col[:, s : s + 1].to_broadcast([P, P]), ident[:])

        def entries(list_tile, slots):
            return list_tile[:, slots.start // STRIPE : slots.stop // STRIPE]

        def vector_gather(dst, window, list_tile, slots):
            nc.vector.tensor_copy(out=dst[:, slots], in_=window[:].indirect(entries(list_tile, slots)))

        def scalar_gather(dst, window, list_tile, slots):
            nc.scalar.activation(out=dst[:, slots], in_=window[:].indirect(entries(list_tile, slots)), func=COPY)

        first = [keep.tile([P, J], F32, name="first%d" % t, align_bytes=64) for t in range(PACK)]
        second = [keep.tile([P, J], F32, name="second%d" % t) for t in range(PACK)]
        larger = {}
        u_rows = [keep.tile([P, J], BF16, name="u_rows%d" % t) for t in range(PACK)]
        turned = [psum.tile([P, len(g), 2, P], F32, name="turned%d" % i) for i, g in enumerate(GROUPS)]
        u_codes = []
        group_plane = [keep.tile([P, len(g) * P], U8, name="u_plane%d" % i, align_bytes=64) for i, g in enumerate(GROUPS)]
        u_plane = [group_plane[i][:, a * P : (a + 1) * P] for i, g in enumerate(GROUPS) for a in range(len(g))]
        turned_of = [turned[i][:, a] for i, g in enumerate(GROUPS) for a in range(len(g))]
        u_in = []

        def x_gather(t, second_gather, slots=ALL_SLOTS):
            scalar_gather(first[t], x_rows[t], list1, slots)
            second_gather(second[t], x_rows[t], list2, slots)

        def x_max(t, tag, slots=ALL_SLOTS):
            tile = keep.tile([P, slots.stop - slots.start], F32, name="larger", tag=tag, align_bytes=64)
            larger[(t, slots.start)] = tile
            nc.vector.tensor_tensor(out=tile[:], in0=first[t][:, slots], in1=second[t][:, slots], op=ALU.max)

        def x_scale(t, slots=ALL_SLOTS):
            quads = slice(slots.start // PACK, slots.stop // PACK)
            nc.vector.scalar_tensor_tensor(
                out=u_rows[t][:, slots].rearrange("p (q s) -> p q s", s=PACK),
                in0=larger[(t, slots.start)][:].rearrange("p (q s) -> p q s", s=PACK),
                scalar=fk_col[:, t : t + 1],
                in1=ra_all[:, :, quads].rearrange("p s q -> p q s"),
                op0=ALU.mult,
                op1=ALU.mult,
            )

        def x_turn(t):
            pairs = u_rows[t][:].bitcast(F32)
            for u in range(2):
                nc.tensor.transpose(turned_of[t][:, u, :], pairs[:, u::2], ident[:])

        def x_leave(i, tag):
            planes = len(GROUPS[i])
            tile = keep.tile([P, planes * P * PACK], BF16, name="u_in", tag=tag, align_bytes=64)
            nc.scalar.copy(
                out=tile[:].bitcast(F32).rearrange("q (a p u) -> q a p u", a=planes, u=2),
                in_=turned[i][:].rearrange("q a u p -> q a p u"),
            )
            u_in.append(tile)

        def x_quantise(i, tag):
            planes = len(GROUPS[i])
            codes = keep.tile([P, planes * P], U32, name="u_codes", tag=tag, align_bytes=64)
            nc.vector.quantize_mx(out=codes[:].bitcast(E4M3), scales=group_plane[i][:], in_=u_in[i][:])
            u_codes.extend([codes[:, a * P : (a + 1) * P] for a in range(planes)])

        picked = [keep.tile([P, J], F32, name="picked%d" % h) for h in range(HALVES)]
        g_in = []
        g_codes = keep.tile([P, N], U32, name="g_codes", align_bytes=64)
        g_plane = keep.tile([P, N], U8, name="g_plane", align_bytes=64)
        g_bank = []

        def g_centre(h, pieces):
            sums = keep.tile([P, J // SET], F32, name="sums%d" % h)
            for slots in pieces:
                nc.vector.tensor_reduce(
                    out=sums[:, slots.start // SET : slots.stop // SET],
                    in_=picked[h][:, slots].rearrange("p (c e) -> p c e", e=SET),
                    axis=mybir.AxisListType.X,
                    op=ALU.add,
                )
            less = keep.tile([P, J // SET, SET // PACK], F32, name="less%d" % h)
            nc.gpsimd.tensor_scalar(
                out=less[:],
                in0=sums[:].unsqueeze(2).to_broadcast([P, J // SET, SET // PACK]),
                scalar1=-1.0 / SET,
                scalar2=0.0,
                op0=ALU.mult,
                op1=ALU.add,
            )
            bank = psum.tile([P, PACK, P], F32, name="g_bank", tag="half%d" % h)
            for s in range(PACK):
                nc.tensor.matmul(
                    bank[:, s, :], lhsT=picked[h][:, s::PACK], rhs=ident[:], is_transpose=True, start=(s == 0), stop=False
                )
            for s in range(PACK):
                nc.tensor.matmul(
                    bank[:, s, :],
                    lhsT=less[:].rearrange("p c e -> p (c e)"),
                    rhs=ident[:],
                    is_transpose=True,
                    start=False,
                    stop=(s == PACK - 1),
                )
            g_bank.append(bank)

        def g_quantise(h):
            cols = slice(h * P, (h + 1) * P)
            nc.vector.quantize_mx(
                out=g_codes[:, cols].bitcast(E5M2), scales=g_plane[:, cols], in_=g_in[h][:].rearrange("q n s -> q (n s)")
            )

        def g_scale(h, tag):
            g_in.append(keep.tile([P, P, PACK], BF16, name="g_in", tag=tag, align_bytes=64))
            nc.vector.tensor_tensor(
                out=g_in[h][:],
                in0=g_bank[h][:].rearrange("q s n -> q n s"),
                in1=rb_col[:].unsqueeze(1).to_broadcast([P, P, PACK]),
                op=ALU.mult,
            )

        early, late = slice(0, LAST_CUT), slice(LAST_CUT, J)
        head, rest = slice(0, G_CUT), slice(G_CUT, J)
        x_gather(0, vector_gather)
        x_max(0, "larger0")
        x_scale(0)
        x_turn(0)
        x_gather(1, scalar_gather)
        for slots in (head, rest):
            vector_gather(picked[0], g_rows[0], list3, slots)
        g_centre(0, (head, rest))
        scalar_gather(picked[1], g_rows[1], list3, ALL_SLOTS)
        x_max(1, "g_rows0")
        g_centre(1, (ALL_SLOTS,))
        x_scale(1)
        x_turn(1)
        g_scale(0, "g_in0")
        x_gather(2, scalar_gather)
        x_gather(3, scalar_gather, early)
        x_gather(3, scalar_gather, late)
        x_max(2, "larger2")
        g_scale(1, "first2")
        x_scale(2)
        x_turn(2)
        x_leave(0, "x_rows3")
        x_max(3, "larger3", early)
        g_quantise(0)
        x_scale(3, early)
        x_max(3, "larger_last", late)
        g_quantise(1)
        x_scale(3, late)
        x_turn(3)
        x_leave(1, "first3")
        old_part = keep.tile([P, R // P, N], F32, name="old_part", tag="fk_col")
        nc.scalar.activation(out=old_part[:], in_=old_rows[:], func=COPY, scale=OUT_SCALE)
        x_quantise(0, "larger_last")
        x_quantise(1, "u_codes1")
        x_leave(2, "u_last")
        x_quantise(2, "u_codes2")

        w_bank = [psum.tile([P, PACK, P], F32, name="w_bank%d" % h) for h in range(HALVES)]
        for t in range(PACK):
            for h in range(HALVES):
                cols = slice(h * P, (h + 1) * P)
                nc.tensor.matmul_mx(
                    out=w_bank[h][:, t, :],
                    lhsT=u_codes[t].bitcast(E4M3),
                    lhsT_scale=u_plane[t],
                    rhs=g_codes[:, cols].bitcast(E5M2),
                    rhs_scale=g_plane[:, cols],
                    start=True,
                    stop=True,
                )
        w_in = [keep.tile([P, P, PACK], BF16, name="w_in%d" % h, align_bytes=64) for h in range(HALVES)]
        nc.vector.tensor_copy(out=w_in[0][:], in_=w_bank[0][:].rearrange("p t n -> p n t"))
        nc.scalar.copy(out=w_in[1][:], in_=w_bank[1][:].rearrange("p t n -> p n t"))
        for h in reversed(range(HALVES)):
            cols = slice(h * P, (h + 1) * P)
            w_codes = keep.tile([P, P], U32, name="w_codes%d" % h, align_bytes=64)
            w_plane = keep.tile([P, P], U8, name="w_plane%d" % h, align_bytes=64)
            nc.vector.quantize_mx(
                out=w_codes[:].bitcast(E5M2), scales=w_plane[:], in_=w_in[h][:].rearrange("p n t -> p (n t)")
            )
            for a in range(R // P):
                rows = slice(a * P, (a + 1) * P)
                v_bank = psum.tile([P, P], F32, name="v_bank", tag=("half%d", "turned%d")[a] % h)
                nc.tensor.matmul_mx(
                    out=v_bank[:],
                    lhsT=dr_codes[:, rows].bitcast(E4M3),
                    lhsT_scale=dr_plane[:, rows],
                    rhs=w_codes[:].bitcast(E5M2),
                    rhs_scale=w_plane[:],
                    start=True,
                    stop=True,
                )
                result = keep.tile([P, P], F32, name="result%d%d" % (h, a))
                nc.vector.scalar_tensor_tensor(
                    out=result[:], in0=v_bank[:], scalar=OUT_SCALE, in1=old_part[:, a, cols], op0=ALU.mult, op1=ALU.max
                )
                (nc.sync, nc.scalar)[a].dma_start(out=out[rows, cols], in_=result[:])
